import numpy as np, ml_dtypes
CORES = [10,34,74,98]
N = 4
import mx_ref
BF = ml_dtypes.bfloat16
def gentries(a):
    return np.ascontiguousarray(a.reshape(8, 16, -1).transpose(0, 2, 1)).reshape(8, -1)
def gtable(e):
    e = np.asarray(e); return np.ascontiguousarray(e.reshape(8, -1, 16).transpose(0, 2, 1)).reshape(128, -1).astype(np.int32)
def gcols(t, e):
    v = np.concatenate([t.reshape(8, 16, -1, 4), np.zeros((8, 16, 1, 4), BF)], axis=2)
    return np.ascontiguousarray(np.stack([v[g][:, e[g]] for g in range(8)])).reshape(128, -1)
def gpick(z, e):
    return np.concatenate([z[16 * g:16 * g + 16][:, e[g]] for g in range(8)])
def tile(rs):
    return np.stack(rs, axis=2).reshape(128, -1).astype(BF)
def pick(q, e):
    c = np.concatenate([q[0].reshape(128, -1, 4), np.zeros((128, 1, 4), np.uint8)], axis=1); s = np.concatenate([q[1], np.ones((16, 1), np.uint8)], axis=1)
    return (np.ascontiguousarray(c[:, e].reshape(128, -1)), np.ascontiguousarray(s[:, e]))
def join(*qs):
    return (np.concatenate([q[0] for q in qs], axis=1), np.concatenate([q[1] for q in qs], axis=1))
def put(q, e, v):
    c, s = q[0].reshape(128, -1, 4).copy(), q[1].copy(); c[:, e] = v[0].reshape(128, -1, 4); s[:, e] = v[1]
    return (c.reshape(128, -1), s)
def pk(c, s):
    return (np.ascontiguousarray(c), mx_ref.live(s))
def emit(q):
    return q[0], q[1]
def packed(v, rng):
    q = [mx_ref.quantize(np.ascontiguousarray(v[r])) for r in range(N)]
    return np.stack([a for a, b in q]), np.stack([mx_ref.plane(b, rng) for a, b in q])
def values_of_codes():
    e, c = np.zeros((128, 128, 4), np.float32), np.zeros((128, 2, 4), np.uint8)
    e[np.arange(128), np.arange(128), 0] = 1
    c[:127, :, 0] = np.arange(256).reshape(2, 128).T[:127]
    return mx_ref.matmul(mx_ref.quantize(e.reshape(128, 512).astype(BF)), (c.reshape(128, 8), np.full((16, 2), 127, np.uint8))).T.reshape(-1).astype(np.float64)
CODE_VALUE, SCALE_VALUE = values_of_codes(), 2.0 ** (np.arange(256) - 127.0)
def decode(q):
    return (CODE_VALUE[q[0]].reshape(16, 8, -1, 4) * SCALE_VALUE[q[1]][:, None, :, None] + 0.0).reshape(128, -1).astype(np.float32)
def f(rng, *shape):
    return mx_ref.flush((rng.standard_normal(shape, dtype=np.float32) * np.exp2(rng.integers(-2, 3, shape[:-1] + (1,)))).astype(BF))
def wide(rng, *shape, cols=0):
    v = rng.standard_normal(shape, dtype=np.float32) * np.exp2(rng.integers(-12, 13, shape)).astype(np.float32)
    if cols: v *= np.repeat(np.exp2(rng.integers(-cols, cols + 1, shape[:-2] + (1, shape[-1] // 4))) * (rng.random(shape[:-2] + (1, shape[-1] // 4)) > 0.0625), 4, axis=-1).astype(np.float32)
    return mx_ref.flush(v.astype(BF))
C, K, A, R, SWEEPS = 384, 160, 64, 3, 4
def big(v):
    v = v.astype(np.float32)
    v[np.abs(v) < np.float32(2.0 ** -16)] = 0
    return v.astype(BF)
def numbers_of(rng):
    return {"x": big(f(rng, N, 128, 4 * C)), "u": np.array(f(rng, N, 128, 512)), "v": np.array(f(rng, N, 128, 512))}
def stored(t):
    return np.stack([gtable(np.clip(t[r], 0, C - 1)) for r in range(N)])
def received(rng):
    return stored(np.arange(C) + rng.integers(-6, 26, (N, 8, C)))
def give(rng, w):
    c, s = packed(np.ascontiguousarray(w).reshape(N, 128, 2048), rng)
    return {"wc": c, "ws": s}
def weights(rng, still=[]):
    w = np.array(mx_ref.flush((rng.standard_normal((N, 128, 2048), dtype=np.float32) * np.float32(0.25)).astype(BF))).reshape(N, 8, 16, 4, 8, 16, 4)
    for i in still:
        w[:, :, i] = 0
        w[:, :, :, :, :, i] = 0
    return give(rng, w)
def setup_inputs(rng):
    return {**numbers_of(rng), "rv": received(rng), **weights(rng)}
def setup_inputs_ties(rng):
    d = numbers_of(rng)
    x = d["x"].reshape(N, 8, 16, C, 4)
    x[:, :, 0] = 0
    x[:, :, 8] = 0
    x[:, :, 0, :, 0] = rng.integers(0, 3, (N, 8, C)).astype(np.float32).astype(BF)
    x[:, :, 8, :, 0] = rng.integers(-1, 2, (N, 8, C)).astype(np.float32).astype(BF)
    u = d["u"].reshape(N, 128, 128, 4)
    u[:, :, ::8] = 0
    o = rng.permutation(N)
    for r in range(N):
        for h in range(0, 128, 16):
            u[r, h, h, 0] = 0.0 if r == o[0] else -1.0 if r == o[1] else 1.0
            u[r, h + 8, h + 8, 0] = 1.0
    t = np.arange(C) + rng.integers(-6, 26, (N, 8, C))
    g = rng.integers(8)
    t[o[0] - 1, g - 1] = 21
    t[o[0], g, C - 1] = 1
    x[o[0], g, 8, C - 1, 0] = 1.0
    return {"x": x.reshape(N, 128, 4 * C), "u": u.reshape(N, 128, 512), "v": d["v"], "rv": stored(t), **weights(rng, [0, 8])}
def setup_inputs_near(rng):
    d = numbers_of(rng)
    x = d["x"].astype(np.float32).reshape(N, 8, 16, C, 4)
    x[:, :, 0] = 0
    x[:, :, 8:] = 0
    x[:, :, 0, :, 0] = rng.integers(0, 2, (N, 8, C)) * 2.0 - 1.0
    s = rng.integers(0, 16, (N, 8, C))
    t = rng.integers(-1, 2, (N, 8, C))
    x[:, :, 8] = ((s[:, :, :, None] >> np.arange(4)) & 1) * np.exp2(np.arange(4) - 23.0)
    x[:, :, 11, :, 0] = 2.0 ** -10
    x[:, :, 12, :, 0] = t * 2.0 ** -10
    u = d["u"].reshape(N, 128, 128, 4)
    u[:, :, ::8] = 0
    u[:, :, 8::16] = 0
    o = rng.permutation(N) % 2
    for r in range(N):
        if o[r] == 1:
            x[r, :, 8:] = 0
            x[r, :, 8, :, 0] = (s[r] - 8) * 2.0 ** -28
            x[r, :, 12, :, 0] = t[r] * 2.0 ** -28
            x[r, :, 13, :, 0] = rng.integers(0, 2, (8, C)) * 1.125 * 2.0 ** -28
            for g in rng.permutation(8)[:4]: x[r, g, 8, rng.integers(C), 0] = 2.0 ** 20 * rng.choice([-1.0, 1.0])
        for h in range(0, 128, 16):
            k = 2.0 ** -30 if o[r] == 1 else 1.0
            u[r, h + 12, h + 8, 0] = k
            if o[r] == 1:
                u[r, h + 8, h, 0] = k
                u[r, h + 13, h, 0] = k
                u[r, h + 13, h + 8, 0] = k
            else:
                u[r, h, h, 0] = k
                u[r, h + 8, h] = k
                u[r, h + 11, h, 0] = k
    return {"x": x.reshape(N, 128, 4 * C).astype(BF), "u": u.reshape(N, 128, 512), "v": d["v"], "rv": received(rng), **weights(rng, [0, 8, 9, 10, 11, 12, 13, 14, 15])}
def setup_inputs_chains(rng):
    d = numbers_of(rng)
    x = d["x"].reshape(N, 8, 16, C, 4)
    m = np.exp2(rng.integers(-12, -5, (N, 8, 8, C, 4))) * (1 + (2 * rng.integers(0, 64, (N, 8, 8, C, 4)) + 1) * 2.0 ** -7) * rng.choice([-1.0, 1.0], (N, 8, 8, C, 4))
    m[:, :, 3, :, 0] = 7.875 * rng.choice([-1.0, 1.0], (N, 8, C))
    x[:, :, :8] = m.astype(np.float32).astype(BF)
    x[:, :, 12] = 0
    x[:, :, 12, :, 0] = np.where(rng.random((N, 8, C)) < 0.0625, -1, 1).astype(np.float32).astype(BF)
    u = d["u"].reshape(N, 128, 128, 4)
    u[:, :, 8::16] = 0
    for h in range(0, 128, 16): u[:, h + 12, h + 8, 0] = 1
    t = np.arange(C) + np.zeros((N, 8, 1), np.int64)
    o = np.repeat(rng.permutation(4), 2) if N == 8 else np.concatenate([[1, 1], rng.permutation([0, 3])])
    o = np.roll(o, rng.integers(N))
    for r in range(N):
        if o[r] == 0: t[r] -= rng.integers(2, 5, (8, 1))
        elif o[r] == 1: t[r, rng.integers(8)] -= 21
        elif o[r] == 2: t[r] = C - 1
        else: t[r] += rng.integers(-30, 61, (8, C))
    return {"x": x.reshape(N, 128, 4 * C), "u": u.reshape(N, 128, 512), "v": d["v"], "rv": stored(t), **weights(rng, [12])}
def setup_inputs_ends(rng):
    d = numbers_of(rng)
    x = np.zeros((N, 8, 16, C, 4))
    u = d["u"].reshape(N, 128, 128, 4)
    w = np.full((N, 128, 2048), 0.25)
    t = np.full((N, 8, C), C - 1)
    i = np.arange(128)
    o = np.roll(np.concatenate([[3, 0], rng.permutation([1, 2])] * (N // 4)), rng.integers(N))
    for r in range(N):
        a = (0.9375 + 0.0625 * rng.integers(0, 2, (8, 16, C, 4))) * 2.0 ** 20
        c = (0.9375 + 0.0625 * rng.integers(0, 2, (128, 128, 4))) * 2.0 ** 30
        if o[r] < 2:
            x[r] = -a
            c[:, 8::16] *= 1.0 if o[r] == 0 else -1.0
            if o[r] == 1: t[r] = 0
            else:
                x[r] = -2.0 ** 20
                z = x[r].reshape(128, C, 4)
                z[:65:8] = 0
                z[:65:8, :, 0] = -((rng.permutation(C) >> np.arange(9)[:, None]) & 1) * np.exp2(11.0 + np.arange(9))[:, None]
                c[:, ::16] = 2.0 ** 30
                for g in rng.permutation(8)[:4]: c[:, 16 * g] *= -1.0
                c[:65:8, ::16, 0] = 2.0 ** 30
                w[r] = 0
                for b in range(4): w[r].reshape(128, 4, 128, 4)[i, b, i, b] = 128.0
            d["v"][r] = 2.0 ** 30
        elif o[r] == 2:
            e = np.arange(C) // 2
            x[r] = (a * rng.choice([-1.0, 1.0], (8, 1, C, 1)))[:, :, e]
            for g in range(8): c[np.arange(128) // 16 != g, 16 * g:16 * g + 16] = 0
            t[r, rng.permutation(8)[:4]] = 0
            d["v"][r] = (2.0 ** 30 * rng.choice([-1.0, 1.0], (128, 512))).astype(np.float32).astype(BF)
        else:
            x[r] = 2.0 ** -28
            c[:] = 2.0 ** -30
            w[r] = 2.0 ** -30
            d["v"][r] = 2.0 ** -30
        u[r] = c.astype(np.float32).astype(BF)
    return {"x": x.reshape(N, 128, 4 * C).astype(np.float32).astype(BF), "u": u.reshape(N, 128, 512), "v": d["v"], "rv": stored(t), **give(rng, w.astype(np.float32).astype(BF))}
def setup_inputs_spread(rng):
    d = setup_inputs(rng)
    d["x"] = big(np.clip(wide(rng, N, 128, 4 * C, cols=6).astype(np.float32), -2.0 ** 20, 2.0 ** 20))
    return d
def check_inputs(d):
    b = []
    for k, lo, hi in (("x", 2.0 ** -28, 2.0 ** 20), ("u", 2.0 ** -30, 2.0 ** 30), ("v", 2.0 ** -30, 2.0 ** 30)):
        a = np.abs(d[k].astype(np.float32))
        if not (np.isfinite(a).all() and ((a == 0) | (a >= lo) & (a <= hi)).all()): b.append("a value of " + k)
    if not ((d["rv"] >= 0) & (d["rv"] < C)).all(): b.append("an entry of rv")
    none, least, most = [emit(mx_ref.quantize(np.full((128, 16), k, np.float32).astype(BF)))[1][0, 0] for k in (0.0, 2.0 ** -30, 2.0 ** 30)]
    for r in range(N):
        if ((d["wc"][r] == 0x7F) | (d["wc"][r] == 0xFF)).any(): b.append("wc: a code that is no number")
        s = mx_ref.live(d["ws"][r])
        if ((s != none) & ((s < least) | (s > most))).any(): b.append("ws: a scale out of range")
        elif not (np.sum(np.abs(decode(pk(d["wc"][r], d["ws"][r])).astype(np.float64)).reshape(128, 512, 4), axis=(0, 2)) <= 128).all(): b.append("a column of W: its sizes")
    return b
def fall(p, b):
    for i in range(SWEEPS): p = np.minimum(p, np.roll(np.take_along_axis(b, p, axis=1), 1, axis=0))
    return p
def mean(a, b):
    return ((a.astype(np.float32) + b.astype(np.float32)) * np.float32(0.5)).astype(BF)
def reference(x, u, v, rv, wc, ws):
    qu = [mx_ref.quantize(u[r]) for r in range(N)]
    lay = [pk(wc[r], ws[r]) for r in range(N)]
    now = [x[r] for r in range(N)]
    p0 = np.zeros((8, 1), np.int64) + A + 2 * np.arange(K)
    lq = np.zeros((N, 8, K), np.float32)
    for t in range(R):
        own, order, bound, sent, line = [], [], [], [], []
        for r in range(N):
            q = mx_ref.quantize(now[r])
            own.append(decode(q).astype(BF))
            s = mx_ref.matmul(qu[r], q) + np.float32(0.0)
            o = np.argsort(-s[::16], axis=1, kind="stable")
            a = np.where(np.take_along_axis(s[8::16], o, axis=1) > 0, np.maximum(gentries(rv[r]) - 1, 0), C - 1)
            a = np.minimum.accumulate(a[:, ::-1], axis=1)[:, ::-1]
            order.append(o)
            bound.append(np.concatenate([a[:, 1:], np.full((8, 1), C - 1)], axis=1))
            line.append(fall(p0, bound[r]))
            sent.append(mx_ref.quantize(mean(gcols(own[r], np.take_along_axis(o, p0, axis=1)), gcols(own[r], np.take_along_axis(o, line[r], axis=1)))))
        for r in range(N):
            e = (r - 1) % N
            p = fall(line[e], bound[r])
            z = mx_ref.quantize(mean(decode(sent[e]), gcols(own[r], np.take_along_axis(order[r], p, axis=1))))
            hit = p[:, None, :] == np.arange(C)[:, None]
            low = np.zeros((8, C), np.int64)
            np.put_along_axis(low, order[r], np.where(hit.any(axis=2), np.argmax(hit, axis=2), K), axis=1)
            new = []
            for b in range(4):
                h = mx_ref.matmul(pick(lay[r], np.arange(128 * b, 128 * b + 128)), z) * np.float32(0.0625)
                new.append(own[r][:, b::4].astype(np.float32) + gpick(np.concatenate([h, np.zeros((128, 1), np.float32)], axis=1), low))
            now[r] = tile(new)
            lq[r] = p
    y = np.zeros((N, 128, C), np.float32)
    oc, osc = np.zeros((N, 128, 4 * C), np.uint8), np.zeros((N, 16, C), np.uint8)
    for r in range(N):
        q = mx_ref.quantize(now[r])
        y[r] = mx_ref.matmul(mx_ref.quantize(v[r]), q)
        oc[r], osc[r] = emit(q)
    return {"y": y, "lq": lq, "oc": oc, "osc": osc}

@@ -1,0 +1,379 @@
+from concourse.mybir import dt, AluOpType, ActivationFunctionType
+
+C, K, R = 384, 160, 3
+DIRECT = (23,)
+MARK = 16
+PART = 96
+XW = 4 * 656
+BIG = 1.0e29
+
+SCRATCH = {
+    "xt": ("sbuf", [128, XW], "bfloat16"), "qx": ("sbuf", [128, C], "float8_e4m3fn_x4"), "sx": ("sbuf", [128, C], "uint8"),
+    "ut": ("sbuf", [128, 512], "bfloat16"), "vt": ("sbuf", [128, 512], "bfloat16"),
+    "qu": ("sbuf", [128, 128], "float8_e4m3fn_x4"), "su": ("sbuf", [128, 128], "uint8"),
+    "qa": ("sbuf", [128, 128], "float8_e4m3fn_x4"), "sa": ("sbuf", [128, 128], "uint8"),
+    "qb": ("sbuf", [128, 128], "float8_e4m3fn_x4"), "sb": ("sbuf", [128, 128], "uint8"),
+    "qv": ("sbuf", [128, 128], "float8_e4m3fn_x4"), "sv": ("sbuf", [128, 128], "uint8"),
+    "wq": ("sbuf", [128, 512], "float8_e4m3fn_x4"), "wp": ("sbuf", [128, 512], "uint8"),
+    "ones": ("sbuf", [128, 2048], "bfloat16"), "et": ("sbuf", [128, 2048], "bfloat16"),
+    "qe": ("sbuf", [128, 512], "float8_e4m3fn_x4"), "se": ("sbuf", [128, 512], "uint8"),
+    "ko": ("sbuf", [128, 512], "bfloat16"), "kot": ("sbuf", [128, 512], "bfloat16"),
+    "qko": ("sbuf", [128, 128], "float8_e4m3fn_x4"), "sko": ("sbuf", [128, 128], "uint8"),
+    "dq": ("sbuf", [128, C], "int32"), "ee": ("sbuf", [128, C], "float32"), "ff": ("sbuf", [128, C], "float32"),
+    "maskb": ("sbuf", [128, C], "float32"), "maskn": ("sbuf", [128, C], "float32"), "ctl": ("sbuf", [128, C], "float32"),
+    "ctlw": ("sbuf", [128, C], "float32"), "cw": ("sbuf", [128, C], "float32"), "jw": ("sbuf", [128, C], "float32"),
+    "kcon": ("sbuf", [128, 24], "float32"), "cols": ("sbuf", [128, 8], "float32"), "r24": ("sbuf", [128, 2], "float32"),
+    "ulf": ("sbuf", [128, 16], "float32"), "ul": ("sbuf", [128, 16], "uint16"),
+    "alf": ("sbuf", [128, 24], "float32"), "al": ("sbuf", [128, 24], "uint16"),
+    "llf": ("sbuf", [128, 10], "float32"), "ll": ("sbuf", [128, 10], "uint16"), "spare": ("sbuf", [128, 10], "int32"),
+    "rvi": ("sbuf", [128, 24], "int32"), "rva": ("sbuf", [128, 24], "float32"),
+    "rflat": ("dram", [8, C], "float32"), "rr": ("sbuf", [128, C], "float32"), "alpha": ("sbuf", [128, C], "float32"),
+    "sm": ("sbuf", [128, C], "float32"), "sw": ("sbuf", [128, C], "float32"),
+    "yy": ("sbuf", [128, 24 * C], "bfloat16"), "rs": ("sbuf", [128, 24 * 192], "bfloat16"),
+    "ra": ("sbuf", [128, 24], "float32"), "cm": ("sbuf", [128, C], "float32"),
+    "run": ("sbuf", [128, 16 + C], "float32"), "rkf": ("sbuf", [128, 24], "float32"), "rl": ("sbuf", [128, 24], "uint16"),
+    "z1": ("sbuf", [128, C], "float32"), "z2": ("sbuf", [128, C], "float32"), "val": ("sbuf", [128, C], "float32"),
+    "w0": ("sbuf", [128, C], "float32"), "wabs": ("sbuf", [128, C], "float32"), "mm": ("sbuf", [128, C], "float32"),
+    "bx": ("sbuf", [128, C], "float32"), "bw": ("sbuf", [128, C], "float32"),
+    "lbf": ("sbuf", [128, 24], "float32"), "lb": ("sbuf", [128, 120], "uint16"),
+    "b4": ("sbuf", [128, K], "float32"), "l4f": ("sbuf", [128, 10], "float32"), "l4": ("sbuf", [128, 32], "uint16"),
+    "kc": ("sbuf", [128, 5 * C], "float32"),
+    "kw": ("sbuf", [128, K], "float32"), "ki": ("sbuf", [128, 10], "int32"), "kj": ("sbuf", [128, 10], "int32"),
+    "lp0": ("sbuf", [128, 10], "uint16"), "lp": ("sbuf", [128, 10], "uint16"), "lv": ("sbuf", [128, 10], "uint16"),
+    "kp": ("sbuf", [128, 10], "int32"), "pk": ("sbuf", [128, K], "float32"), "pl": ("sbuf", [128, K], "float32"),
+    "qk0": ("sbuf", [128, K], "float32"), "qk1": ("sbuf", [128, K], "float32"), "qk": ("sbuf", [128, K + 8], "float32"),
+    "kw2": ("sbuf", [128, K], "float32"), "kn": ("sbuf", [128, 10], "int32"), "kq": ("sbuf", [128, 10], "int32"),
+    "ds": ("sbuf", [128, 10], "int32"), "dl": ("sbuf", [128, 40], "uint16"),
+    "qi": ("sbuf", [128, K], "int32"), "qf": ("sbuf", [128, K], "float32"), "qo": ("sbuf", [128, K], "float32"),
+    "fh": ("sbuf", [128, 4 * C], "bfloat16"), "fu": ("sbuf", [128, 4 * C], "bfloat16"),
+    "fp0": ("sbuf", [128, 4 * K], "bfloat16"), "etile": ("sbuf", [128, 4 * K], "bfloat16"),
+    "vtile": ("sbuf", [128, 4 * K], "bfloat16"), "qz": ("sbuf", [128, K], "float8_e4m3fn_x4"), "sz": ("sbuf", [128, K], "uint8"),
+    "de": ("sbuf", [128, 4 * K], "float32"), "h16": ("sbuf", [128, 4 * K], "float32"), "nt": ("sbuf", [128, 4 * K], "bfloat16"),
+    "yo": ("sbuf", [128, C], "float32"),
+    "pa": ("psum", [128, 2048], "float32"), "pb": ("psum", [128, 2048], "float32"),
+}
+TILES = [(384, (0, 23, 22, 21)), (320, (20, 19, 18, 17)), (256, (16, 15, 14, 13)), (192, (12, 11, 10, 9)), (128, (8, 7, 6, 5)), (128, (4, 3, 2, 1))]
+for _q, (_n, _s) in enumerate(TILES):
+    SCRATCH["mt%d" % _q] = ("sbuf", [128, 4 * _n], "bfloat16")
+    SCRATCH["qm%d" % _q] = ("sbuf", [128, _n], "float8_e4m3fn_x4")
+    SCRATCH["sm%d" % _q] = ("sbuf", [128, _n], "uint8")
+SCRATCH["ec"] = SCRATCH["lc"] = ("sbuf", [128, R * K], "float8_e4m3fn_x4")
+SCRATCH["es"] = SCRATCH["ls"] = ("sbuf", [128, R * K], "uint8")
+SCRATCH["po"] = SCRATCH["pi"] = ("sbuf", [128, R * 56], "uint16")
+
+SEMAPHORES = ["v", "s", "t", "p", "dx", "du", "dw", "dv", "drv", "drf", "drr", "dout", "ls"]
+SEMAPHORES += ["%s%d" % (a, t) for a in ("ae", "ap", "rc", "rp") for t in range(R)]
+SEMAPHORES += ["rb%d%d" % (t, m) for t in range(R) for m in range(1, 5)]
+
+
+def rank_program(g, core, T, topo):
+    rank = T.rank_of(core)
+    if rank is None:
+        return
+    A, F = AluOpType, ActivationFunctionType
+    eng = {"v": g.vector, "s": g.scalar, "t": g.tensor, "p": g, "y": g.sync}
+    cnt, seen = {}, {}
+
+    def need(q, toks):
+        best = {}
+        for k in toks:
+            if k is not None:
+                best[k[0]] = max(best.get(k[0], 0), k[1])
+        for s, n in best.items():
+            if seen.get((q, s), 0) < n:
+                eng[q].wait_ge(T.sem[s], n)
+                seen[(q, s)] = n
+
+    def done(ins, sem, n=1):
+        ins.then_inc(T.sem[sem], n)
+        cnt[sem] = cnt.get(sem, 0) + n
+        return (sem, cnt[sem])
+
+    def all_of(sem):
+        return (sem, cnt[sem])
+
+    def copy(deps, out, in_):
+        need("v", deps)
+        return done(g.vector.tensor_copy(out, in_), "v")
+
+    def tt(deps, out, a, b, op):
+        need("v", deps)
+        return done(g.vector.tensor_tensor(out, a, b, op), "v")
+
+    def ts(deps, out, a, s1, s2, op0, op1=None):
+        need("v", deps)
+        if op1 is None:
+            return done(g.vector.tensor_scalar(out, a, s1, None, op0), "v")
+        return done(g.vector.tensor_scalar(out, a, s1, s2, op0, op1), "v")
+
+    def scan(deps, out, d0, d1, init, op0, op1):
+        need("v", deps)
+        return done(g.vector.tensor_tensor_scan(out, d0, d1, init, op0, op1), "v")
+
+    def fill(deps, out, c):
+        need("v", deps)
+        return done(g.vector.memset(out, c), "v")
+
+    def quant(deps, q, s, x):
+        need("v", deps)
+        return done(g.vector.quantize_mx(q, s, x), "v")
+
+    def act(deps, out, in_, func=None, bias=0.0, scale=1.0):
+        need("s", deps)
+        f = F.Copy if func is None else func
+        if func is None and scale == 1.0:
+            return done(g.scalar.activation(out, in_, f), "s")
+        if func is None:
+            return done(g.scalar.activation(out, in_, f, scale=scale), "s")
+        return done(g.scalar.activation(out, in_, f, bias=bias, scale=scale), "s")
+
+    def mm(deps, out, w, ws, x, xs, start=True, stop=True):
+        need("t", deps)
+        return done(g.tensor.matmul_mx(out, w, ws, x, xs, start, stop), "t")
+
+    def iota(out, pattern, base, cm):
+        return done(g.iota(out, pattern, base, cm, allow_small_or_imprecise_dtypes=True), "p")
+
+    def dma(q, deps, out, in_, sem):
+        need(q, deps)
+        return done(eng[q].dma_start(out, in_), sem, 16)
+
+    def rotate(deps, buf, w, sem, o=0, each=False):
+        tok = []
+        for m in range(1, 5):
+            z, d = sem + (str(m) if each else ""), o + w * m
+            dma("y", deps, buf[16 * m:128, d:d + w], buf[0:128 - 16 * m, o:o + w], z)
+            tok.append(dma("s", deps, buf[0:16 * m, d:d + w], buf[128 - 16 * m:128, o:o + w], z))
+        return tok
+
+    def segments(deps, scratch, src, out):
+        n = 16 * out.shape[1]
+        a = scan(deps, scratch[:, 0:n], src, T.ctlw[:, 0:n], 1.0e6, A.min, A.max)
+        return tt([a], out, scratch[:, 7:n:16], scratch[:, 15:n:16], A.min)
+
+    t_u = dma("s", [], T.ut[:], T.u[:], "du")
+    t_x = dma("y", [], T.xt[:, 0:4 * C], T.x[:], "dx")
+    t_rv = dma("s", [], T.rvi[:], T.rv[:], "drv")
+    dma("y", [], T.wq[:].bitcast(dt.uint8), T.wc[:], "dw")
+    t_w = dma("y", [], T.wp[:], T.ws[:], "dw")
+    t_vi = dma("y", [], T.vt[:], T.v[:], "dv")
+
+    c_ul = iota(T.ulf[:], [[8, 2], [16, 8]], 0, 0)
+    c_dq = iota(T.dq[:], [[1, C]], 128, -1)
+    c_ee = iota(T.ee[:], [[0, 24], [1, 16]], 0, 0)
+    c_kc = iota(T.kcon[:], [[-16, 24]], 575, 0)
+    v_one = fill([], T.ones[:], 1.0)
+    need("p", [v_one])
+    a = done(g.affine_select(T.kot[:], T.ones[:, 0:512], [[-16, 8], [0, 64]], A.is_ge, 0.0, 0, 1), "p")
+    need("p", [a])
+    c_ko = done(g.affine_select(T.ko[:], T.kot[:], [[16, 8], [0, 64]], A.is_ge, 0.0, 15, -1), "p")
+    c_al = iota(T.alf[:], [[-1, 24]], 23, 0)
+    c_ll = iota(T.llf[:], [[-16, 10]], 144, 0)
+    c_sp = iota(T.spare[:], [[16, 10]], C, 1)
+    c_cw = iota(T.cw[:], [[1, C]], 512, 0)
+    c_et = done(g.affine_select(T.et[:], T.ones[:], [[-1, 4], [1, 512]], A.is_equal, 0.0, 0, -4), "p")
+    c_jw = iota(T.jw[:], [[512, C]], -512, 0)
+
+    v_ul = copy([c_ul], T.ul[:], T.ulf[:])
+    v_dq = ts([c_dq], T.dq[:], T.dq[:], 15, None, A.bitwise_and)
+    v_mb = ts([v_dq], T.maskb[:], T.dq[:], 0.5, -2.0 * BIG, A.subtract, A.mult)
+    v_c0 = copy([v_dq], T.cols[:, 0:1], T.dq[:, 15:16])
+    v_qu = quant([t_u], T.qu[:], T.su[:], T.ut[:])
+    for q, s, a in ((T.qa, T.sa, 0), (T.qb, T.sb, 8)):
+        v_pick = copy([v_qu, v_ul], q[:].bitcast(dt.uint32), T.qu[:].bitcast(dt.uint32).indirect(T.ul[:, a:a + 8]))
+        s_pick = act([v_qu, v_ul], s[:], T.su[:].indirect(T.ul[:, a:a + 8]))
+    v_qx = quant([t_x], T.qx[:], T.sx[:], T.xt[:, 0:4 * C])
+    v_ct = ts([c_ee], T.ctl[:], T.ee[:], 0.5, 2.0 * BIG, A.subtract, A.mult)
+    late = {}
+
+    def constants_early():
+        for q, (n, segs) in enumerate(TILES):
+            late["mz"] = fill([], T["mt%d" % q][:, 64 * min(k for k in segs if k):4 * n], 0.0)
+        fill([], T.rs[:, 191:192], -192.0)
+        late["run"] = fill([], T.run[:, 0:16], 0.0)
+        late["kc"] = ts([v_c0, c_kc], T.kcon[:], T.kcon[:], T.cols[:, 0:1], None, A.subtract)
+        a = ts([t_rv], T.rva[:], T.rvi[:], 1.0, 384.0, A.max, A.subtract)
+        a = ts([a], T.rva[:], T.rva[:], -1.0, None, A.mult)
+        t_rf = dma("y", [a], T.rflat[:], T.rva[:], "drf")
+        for q in range(16):
+            dma("y", [t_rf], T.rr[q:128:16, :], T.rflat[:], "drr")
+        a = ts([], T.cols[:, 1:2], T.cols[:, 0:1], -1.0, 15.0, A.mult, A.add)
+        b = ts([a], T.cols[:, 2:3], T.cols[:, 1:2], 8.0, 8.0, A.is_ge, A.mult)
+        c = tt([b], T.cols[:, 3:4], T.cols[:, 2:3], T.cols[:, 1:2], A.add)
+        d = tt([b], T.cols[:, 4:5], T.cols[:, 2:3], T.cols[:, 1:2], A.subtract)
+        ts([c], T.cols[:, 5:6], T.cols[:, 3:4], -0.5, -3.5, A.mult, A.add)
+        late["b2"] = ts([d], T.cols[:, 6:7], T.cols[:, 4:5], -0.5e6, -3.75e6, A.mult, A.add)
+        a = ts([], T.r24[:, 0:1], T.cols[:, 0:1], 24.0, None, A.mult)
+        late["ar"] = ts([a, c_al], T.al[:], T.alf[:], T.r24[:, 0:1], None, A.add)
+        late["ko"] = quant([c_ko], T.qko[:], T.sko[:], T.ko[:])
+        late["mn"] = ts([v_dq], T.maskn[:], T.dq[:], 0.0, -1.0, A.is_equal, A.mult)
+
+    nxt = T.cores[(rank + 1) % len(T.cores)]
+    rid, pid = topo.addr(nxt)[0:2]
+    mask, ne = topo.mask(core, nxt), len(topo.engines(core, nxt))
+
+    def send(deps, out, in_, sem):
+        need("p", deps)
+        g.remote_dma(out, in_, T.sem[sem], T.sem.ls, pid, rid, mask)
+        cnt["ls"] = cnt.get("ls", 0) + ne
+        cnt[sem] = cnt.get(sem, 0) + ne
+
+    t_h = t_de = None
+    for t in range(R):
+        last = t == R - 1
+        p_s1 = mm([v_qx, v_pick, s_pick, t_de], T.pb[:, 0:C], T.qa[:], T.sa[:], T.qx[:], T.sx[:])
+        p_s2 = mm([], T.pb[:, 512:512 + C], T.qa[:], T.sa[:], T.qx[:], T.sx[:])
+        p_mk = mm([], T.pb[:, 1024:1024 + C], T.qb[:], T.sb[:], T.qx[:], T.sx[:])
+        a = tt([p_s1, v_mb], T.sm[:], T.pb[:, 0:C], T.maskb[:], A.min)
+        v_sw = scan([a, v_ct], T.sw[:], T.ctl[:], T.sm[:], -BIG, A.min, A.max)
+        if t == 0:
+            constants_early()
+        y = {}
+        for i, k in enumerate(k for n, segs in TILES for k in segs if k):
+            if i == MARK:
+                a = act([p_mk], T.z1[:], T.pb[:, 1024:1024 + C], F.Sign)
+                s_z = act([a], T.z2[:], T.z1[:], F.Sign, -1.0, 2.0)
+            if k in DIRECT:
+                continue
+            y[k] = act([p_s2, v_sw], T.yy[:, C * k:C * k + 16 * k], T.pb[:, 512:512 + 16 * k], F.Sign, T.sw[:, 16 * k + 15:16 * k + 16], -1.0)
+        if t == 0:
+            a = act([late["b2"], c_ee], T.ff[:], T.ee[:], F.Abs, T.cols[:, 5:6])
+            late["cw"] = act([a], T.ctlw[:], T.ff[:], F.Identity, T.cols[:, 6:7], 1.0e6)
+            late["al"] = act([late["ar"], all_of("drr")], T.alpha[:], T.rr[:].indirect(T.al[:]))
+        pending = []
+
+        def flush():
+            while pending:
+                m, e, k, tok = pending.pop()
+                late["rs"] = scan(tok, T.rs[:, 192 * k + 192 - 8 * k:192 * k + 192], m[:, e:32 * k:4], m[:, 32 * k + e:64 * k:4], -192.0, A.add, A.add)
+
+        for q, (n, segs) in enumerate(TILES):
+            m, ok = T["mt%d" % q], [late["mz"]]
+            for e, k in enumerate(segs):
+                if k == 0:
+                    ok.append(tt([v_sw], m[:, 0:4 * C:4], T.pb[:, 0:C], T.sw[:], A.is_le))
+                    v_md = ok[-1]
+                    continue
+                if k in DIRECT:
+                    a = ts([v_sw], m[:, e:64 * k:4], T.pb[:, 0:16 * k], T.sw[:, 16 * k + 15:16 * k + 16], None, A.is_lt)
+                else:
+                    a = ts([y[k]], m[:, e:64 * k:4], T.yy[:, C * k:C * k + 16 * k], 0.0, None, A.is_gt)
+                ok.append(a)
+                flush()
+                pending.append((m, e, k, [a]))
+            if q == 5:
+                flush()
+            v_qm = quant(ok, T["qm%d" % q][:], T["sm%d" % q][:], m[:])
+            p_col = mm([v_qm, late["ko"], t_de], T.pb[:, 1536:1536 + n], T.qko[:], T.sko[:], T["qm%d" % q][:], T["sm%d" % q][:], q == 0, q == 5)
+        v_ra = tt([late["rs"], late["kc"]], T.ra[:], T.rs[:, 191:24 * 192:192], T.kcon[:], A.add)
+        v_val = tt([s_z, c_cw], T.val[:], T.z2[:], T.cw[:], A.mult)
+        a = tt([p_col, late["mn"]], T.cm[:], T.pb[:, 1536:1536 + C], T.maskn[:], A.mult)
+        a = scan([a, v_md, late["run"]], T.run[:, 16:16 + C], T.cm[:], T.mt0[:, 0:4 * C:4], 0.0, A.add, A.add)
+        a = tt([a], T.rkf[:], T.run[:, 31:16 + C:16], T.run[:, 15:C:16], A.subtract)
+        a = tt([a, v_ra], T.rkf[:], T.rkf[:], T.ra[:], A.add)
+        v_rl = copy([a], T.rl[:], T.rkf[:])
+        if t == 0:
+            late["qe"] = quant([c_et], T.qe[:], T.se[:], T.et[:])
+            fill([], T.bx[:, 0:1], 0.0)
+            late["bz"] = fill([], T.qk[:, K:K + 8], 9.0e5)
+        p_f = [mm([late["qe"], t_h], T.pa[:, 512 * b:512 * b + C], T.qe[:, 128 * b:128 * b + 128], T.se[:, 128 * b:128 * b + 128], T.qx[:], T.sx[:]) for b in range(4)]
+        v_w0 = copy([v_rl, v_val], T.w0[:].indirect(T.rl[:]), T.val[:])
+        a = tt([v_w0, late["al"]], T.mm[:], T.w0[:], T.alpha[:], A.min)
+        v_bx = scan([a], T.bx[:, 1:C], T.mm[:, 0:C - 1], T.mm[:, 0:C - 1], 0.0, A.max, A.max)
+        a = segments([v_bx, late["bz"], late["cw"]], T.bw, T.bx[:], T.lbf[:])
+        v_lb = copy([a], T.lb[:, 0:24], T.lbf[:])
+        s_fh = [act([p_f[b]], T.fh[:, C * b:C * b + C], T.pa[:, 512 * b:512 * b + C], None, 0.0, 0.5) for b in range(4)]
+        s_wa = act([v_w0], T.wabs[:], T.w0[:], F.Abs)
+        d_lb = rotate([v_lb], T.lb, 24, "rb%d" % t, 0, True)
+        a = segments([v_bx], T.b4, T.bx[:, 1:321:2], T.l4f[:])
+        v_l4 = copy([a], T.l4[:, 0:10], T.l4f[:])
+        dma("y", [v_l4], T.l4[64:128, 16:26], T.l4[0:64, 0:10], "rc%d" % t)
+        d_l4 = dma("s", [v_l4], T.l4[0:64, 16:26], T.l4[64:128, 0:10], "rc%d" % t)
+        v_k0 = tt([s_wa, c_jw], T.kc[:, 0:C], T.wabs[:], T.jw[:], A.add)
+        a = segments([v_k0], T.kw, T.kc[:, 1:321:2], T.ki[:])
+        a = ts([a], T.kj[:], T.ki[:], 511, None, A.bitwise_and)
+        v_l0 = copy([a], T.lp0[:], T.kj[:])
+        f0 = []
+        for b in range(4):
+            w, o = T.fh[:, C * b:C * b + C].indirect(T.lp0[:]), T.fp0[:, K * b:K * b + K]
+            f0.append(copy([v_l0, s_fh[b]], o, w) if b < 2 else act([v_l0, s_fh[b]], o, w))
+        acc = T.kc[:, 1:321:2]
+        s_kc = v_kc = before = v_k0
+        v_p = None
+        for m in range(1, 5):
+            pt = PART if m < 4 else 0
+            w, l = T.kc[:, C * (m - 1):C * m], 24 * m
+            if pt:
+                v_kc = copy([d_lb[m - 1], s_kc, v_kc], T.kc[:, C * m:C * m + pt], w.indirect(T.lb[:, l:l + pt // 16]))
+            s_kc = act([d_lb[m - 1], s_kc, before], T.kc[:, C * m + pt:C * m + C], w.indirect(T.lb[:, l + pt // 16:l + 24]))
+            before = v_kc
+            if m < 4:
+                v_p = tt([s_kc, v_kc, v_p], T.pk[:], acc, T.kc[:, C * m + 1:C * m + 321:2], A.max)
+                acc = T.pk[:]
+            if m == 3:
+                v_p = tt([v_p, d_l4], T.pl[:], T.kc[:, C * m:C * m + C].indirect(T.l4[:, 16:26]), T.pk[:], A.max)
+        k0, l0 = K * t, 56 * t
+        ec, es, lc, ls = [T[k][:, k0:k0 + K] for k in ("ec", "es", "lc", "ls")]
+        v_k = segments([v_p], T.kw, T.pl[:], T.ki[:])
+        a = ts([v_k], T.kp[:], T.ki[:], 9, None, A.arith_shift_right)
+        v_po = copy([a], T.po[:, l0:l0 + 10], T.kp[:])
+        d_po = rotate([v_po], T.po, 10, "rp%d" % t, l0)[3]
+        a = ts([v_k], T.kj[:], T.ki[:], 511, None, A.bitwise_and)
+        v_lp = copy([a], T.lp[:], T.kj[:])
+        e = [tt([v_lp, f0[b]], T.etile[:, b:4 * K:4], T.fh[:, C * b:C * b + C].indirect(T.lp[:]), T.fp0[:, K * b:K * b + K], A.add) for b in range(4)]
+        v_ec = quant(e, ec, es, T.etile[:])
+        send([v_ec], lc.bitcast(dt.uint8), ec.bitcast(dt.uint8), "ae%d" % t)
+        send([d_po], T.pi[:, l0:l0 + 50], T.po[:, l0:l0 + 50], "ap%d" % t)
+        send([], ls, es, "ae%d" % t)
+        if t == 0:
+            late["ll"] = ts([c_ll, v_c0], T.ll[:], T.llf[:], T.cols[:, 0:1], None, A.add)
+            late["qv"] = quant([t_vi], T.qv[:], T.sv[:], T.vt[:])
+        s_fu = [act([p_f[b]], T.fu[:, C * b:C * b + C], T.pa[:, 512 * b:512 * b + C]) for b in range(4)]
+        s_xb = [act([p_f[b], v_qx], T.xt[:, b:4 * C:4], T.pa[:, 512 * b:512 * b + C]) for b in range(4)]
+        a = copy([all_of("ap%d" % t), s_kc, v_kc], T.qk0[:], T.kc[:, 0:C].indirect(T.pi[:, l0:l0 + 10]))
+        src = T.qk0
+        for m in range(1, 5):
+            dst = T.qk if m == 4 else (T.qk1, T.qk0)[(m - 1) % 2]
+            a = tt([a], dst[:, 0:K], T.kc[:, C * m:C * m + C].indirect(T.pi[:, l0 + 10 * m:l0 + 10 * m + 10]), src[:, 0:K], A.max)
+            src = dst
+        v_qk = a
+        v_kq = segments([v_qk], T.kw, T.qk[:, 0:K], T.kq[:])
+        v_oq = ts([v_kq], T.kj[:], T.kq[:], 511, None, A.bitwise_and)
+        v_lv = copy([v_oq], T.lv[:], T.kj[:])
+        z = []
+        for b in range(4):
+            p_d = mm([all_of("ae%d" % t), v_val, v_rl], T.pb[:, 512 * b:512 * b + K], T.qe[:, 128 * b:128 * b + 128], T.se[:, 128 * b:128 * b + 128], lc, ls)
+            t_de = act([p_d], T.de[:, K * b:K * b + K], T.pb[:, 512 * b:512 * b + K], None, 0.0, 0.5)
+            z.append(tt([v_lv, t_de], T.vtile[:, b:4 * K:4], T.fh[:, C * b:C * b + C].indirect(T.lv[:]), T.de[:, K * b:K * b + K], A.add))
+        v_z = quant(z, T.qz[:], T.sz[:], T.vtile[:])
+        h = []
+        for b in range(4):
+            p_h = mm([v_z, t_w, s_xb[3]], T.pa[:, 512 * b:512 * b + K], T.wq[:, 128 * b:128 * b + 128], T.wp[:, 128 * b:128 * b + 128], T.qz[:], T.sz[:])
+            t_h = act([p_h], T.h16[:, K * b:K * b + K], T.pa[:, 512 * b:512 * b + K], None, 0.0, 0.0625)
+            h.append(t_h)
+        v_kn = segments([v_qk, late["bz"]], T.kw2, T.qk[:, 1:K + 1], T.kn[:])
+        a = tt([v_kn, v_kq], T.kn[:], T.kq[:], T.kn[:], A.is_equal)
+        b_ = tt([v_oq, c_sp], T.ds[:], T.spare[:], T.kj[:], A.subtract)
+        a = tt([a, b_], T.ds[:], T.ds[:], T.kn[:], A.mult)
+        a = tt([a], T.ds[:], T.ds[:], T.kj[:], A.add)
+        d = [ts([a], T.dl[:, 10 * b:10 * b + 10], T.ds[:], 4.0, float(b), A.mult, A.add) for b in range(4)]
+        v_xs = None
+        n_ = [tt([v_lv, h[b], s_fu[b]], T.nt[:, K * b:K * b + K], T.fu[:, C * b:C * b + C].indirect(T.lv[:]), T.h16[:, K * b:K * b + K], A.add) for b in range(4)]
+        for b in range(4):
+            v_xs = copy([n_[b], d[b], s_xb[3], v_xs], T.xt[:].indirect(T.dl[:, 10 * b:10 * b + 10]), T.nt[:, K * b:K * b + K])
+        v_qx = quant([v_xs, p_f[3]], T.qx[:], T.sx[:], T.xt[:, 0:4 * C])
+        if last:
+            a = copy([v_qk], T.qi[:], T.qk[:, 0:K])
+            a = ts([a], T.qi[:], T.qi[:], 9, None, A.arith_shift_right)
+            a = ts([a], T.qf[:], T.qi[:], -1.0, 383.0, A.mult, A.add)
+            v_lq = copy([a, late["ll"]], T.qo[:], T.qf[:].indirect(T.ll[:]))
+
+    dma("y", [v_qx], T.oc[:], T.qx[:].bitcast(dt.uint8), "dout")
+    for k in range(4):
+        dma("s" if k % 2 else "y", [v_qx], T.osc[4 * k:4 * k + 4, :], T.sx[32 * k:32 * k + 4, :], "dout")
+    p_y = mm([v_qx, late["qv"], t_de], T.pb[:, 0:C], T.qv[:], T.sv[:], T.qx[:], T.sx[:])
+    s_y = act([p_y], T.yo[:], T.pb[:, 0:C])
+    for q in range(8):
+        dma("y", [v_lq], T.lq[q:q + 1, :], T.qo[16 * q:16 * q + 1, :], "dout")
+    dma("s", [s_y], T.y[:], T.yo[:], "dout")
+    need("p", [all_of(s) for s in cnt])

@@ -62,8 +62,8 @@ SCRATCH["es"] = SCRATCH["ls"] = ("sbuf", [128, R * K], "uint8")
 SCRATCH["po"] = SCRATCH["pi"] = ("sbuf", [128, R * 56], "uint16")
 
 SEMAPHORES = ["v", "s", "t", "p", "dx", "du", "dw", "dv", "drv", "drf", "drr", "dout", "ls"]
-SEMAPHORES += ["%s%d" % (a, t) for a in ("ae", "ap", "rc", "rp") for t in range(R)]
-SEMAPHORES += ["rb%d%d" % (t, m) for t in range(R) for m in range(1, 5)]
+SEMAPHORES += ["%s%d" % (a, t) for a in ("ae", "ap", "rc") for t in range(R)]
+SEMAPHORES += ["%s%d%d" % (a, t, m) for a in ("rb", "rp") for t in range(R) for m in range(1, 5)]
 
 
 def rank_program(g, core, T, topo):
@@ -163,6 +163,14 @@ def rank_program(g, core, T, topo):
     c_ee = iota(T.ee[:], [[0, 24], [1, 16]], 0, 0)
     c_kc = iota(T.kcon[:], [[-16, 24]], 575, 0)
     v_one = fill([], T.ones[:], 1.0)
+    late = {}
+    for q, (n, segs) in enumerate(TILES):
+        o, w = 64 * min(k for k in segs if k), 4 * n
+        act([v_one], T["mt%d" % q][:, o:w], T.ones[:, o:w], None, 0.0, 0.0)
+    act([], T.rs[:, 191:192], T.ones[:, 0:1], None, 0.0, -192.0)
+    act([], T.run[:, 0:16], T.ones[:, 0:16], None, 0.0, 0.0)
+    act([], T.bx[:, 0:1], T.ones[:, 0:1], None, 0.0, 0.0)
+    late["mz"] = act([], T.qk[:, K:K + 8], T.ones[:, 0:8], None, 0.0, 9.0e5)
     need("p", [v_one])
     a = done(g.affine_select(T.kot[:], T.ones[:, 0:512], [[-16, 8], [0, 64]], A.is_ge, 0.0, 0, 1), "p")
     need("p", [a])
@@ -172,11 +180,12 @@ def rank_program(g, core, T, topo):
     c_sp = iota(T.spare[:], [[16, 10]], C, 1)
     c_cw = iota(T.cw[:], [[1, C]], 512, 0)
     c_et = done(g.affine_select(T.et[:], T.ones[:], [[-1, 4], [1, 512]], A.is_equal, 0.0, 0, -4), "p")
-    c_jw = iota(T.jw[:], [[512, C]], -512, 0)
+    c_jw = iota(T.jw[:], [[1024, C]], -512, 0)
 
     v_ul = copy([c_ul], T.ul[:], T.ulf[:])
     v_dq = ts([c_dq], T.dq[:], T.dq[:], 15, None, A.bitwise_and)
     v_mb = ts([v_dq], T.maskb[:], T.dq[:], 0.5, -2.0 * BIG, A.subtract, A.mult)
+    late["mn"] = ts([v_dq], T.maskn[:], T.dq[:], 0.0, None, A.is_equal)
     v_c0 = copy([v_dq], T.cols[:, 0:1], T.dq[:, 15:16])
     v_qu = quant([t_u], T.qu[:], T.su[:], T.ut[:])
     for q, s, a in ((T.qa, T.sa, 0), (T.qb, T.sb, 8)):
@@ -184,29 +193,29 @@ def rank_program(g, core, T, topo):
         s_pick = act([v_qu, v_ul], s[:], T.su[:].indirect(T.ul[:, a:a + 8]))
     v_qx = quant([t_x], T.qx[:], T.sx[:], T.xt[:, 0:4 * C])
     v_ct = ts([c_ee], T.ctl[:], T.ee[:], 0.5, 2.0 * BIG, A.subtract, A.mult)
-    late = {}
 
     def constants_early():
-        for q, (n, segs) in enumerate(TILES):
-            late["mz"] = fill([], T["mt%d" % q][:, 64 * min(k for k in segs if k):4 * n], 0.0)
-        fill([], T.rs[:, 191:192], -192.0)
-        late["run"] = fill([], T.run[:, 0:16], 0.0)
-        late["kc"] = ts([v_c0, c_kc], T.kcon[:], T.kcon[:], T.cols[:, 0:1], None, A.subtract)
+        k = [T.cols[:, i:i + 1] for i in range(8)]
+        r = act([v_c0], k[1], k[0], F.Identity, 15.0, -1.0)
+        late["ar"] = act([], T.r24[:, 0:1], k[0], None, 0.0, 24.0)
+        a = act([], k[7], k[0], None, 0.0, -1.0)
+        late["kc"] = act([a, c_kc], T.kcon[:], T.kcon[:], F.Identity, k[7])
+        a = act([r], k[2], k[1], F.Sign, -7.5)
+        a = act([a], k[3], k[2], F.Identity, 4.0, 4.0)
+        b = act([a], k[4], k[3], F.Identity, k[1])
+        c = act([a], k[5], k[1], F.Identity, k[3], -1.0)
+        b = act([b], k[2], k[4], F.Identity, -3.5, -0.5)
+        c = act([c], k[6], k[5], F.Identity, -3.75e6, -0.5e6)
+        late["b"] = c
+
+    def constants_lists():
         a = ts([t_rv], T.rva[:], T.rvi[:], 1.0, 384.0, A.max, A.subtract)
         a = ts([a], T.rva[:], T.rva[:], -1.0, None, A.mult)
         t_rf = dma("y", [a], T.rflat[:], T.rva[:], "drf")
         for q in range(16):
             dma("y", [t_rf], T.rr[q:128:16, :], T.rflat[:], "drr")
-        a = ts([], T.cols[:, 1:2], T.cols[:, 0:1], -1.0, 15.0, A.mult, A.add)
-        b = ts([a], T.cols[:, 2:3], T.cols[:, 1:2], 8.0, 8.0, A.is_ge, A.mult)
-        c = tt([b], T.cols[:, 3:4], T.cols[:, 2:3], T.cols[:, 1:2], A.add)
-        d = tt([b], T.cols[:, 4:5], T.cols[:, 2:3], T.cols[:, 1:2], A.subtract)
-        ts([c], T.cols[:, 5:6], T.cols[:, 3:4], -0.5, -3.5, A.mult, A.add)
-        late["b2"] = ts([d], T.cols[:, 6:7], T.cols[:, 4:5], -0.5e6, -3.75e6, A.mult, A.add)
-        a = ts([], T.r24[:, 0:1], T.cols[:, 0:1], 24.0, None, A.mult)
-        late["ar"] = ts([a, c_al], T.al[:], T.alf[:], T.r24[:, 0:1], None, A.add)
+        late["ar"] = ts([late["ar"], c_al], T.al[:], T.alf[:], T.r24[:, 0:1], None, A.add)
         late["ko"] = quant([c_ko], T.qko[:], T.sko[:], T.ko[:])
-        late["mn"] = ts([v_dq], T.maskn[:], T.dq[:], 0.0, -1.0, A.is_equal, A.mult)
 
     nxt = T.cores[(rank + 1) % len(T.cores)]
     rid, pid = topo.addr(nxt)[0:2]
@@ -228,6 +237,7 @@ def rank_program(g, core, T, topo):
         v_sw = scan([a, v_ct], T.sw[:], T.ctl[:], T.sm[:], -BIG, A.min, A.max)
         if t == 0:
             constants_early()
+            constants_lists()
         y = {}
         for i, k in enumerate(k for n, segs in TILES for k in segs if k):
             if i == MARK:
@@ -237,7 +247,7 @@ def rank_program(g, core, T, topo):
                 continue
             y[k] = act([p_s2, v_sw], T.yy[:, C * k:C * k + 16 * k], T.pb[:, 512:512 + 16 * k], F.Sign, T.sw[:, 16 * k + 15:16 * k + 16], -1.0)
         if t == 0:
-            a = act([late["b2"], c_ee], T.ff[:], T.ee[:], F.Abs, T.cols[:, 5:6])
+            a = act([late["b"], c_ee], T.ff[:], T.ee[:], F.Abs, T.cols[:, 2:3])
             late["cw"] = act([a], T.ctlw[:], T.ff[:], F.Identity, T.cols[:, 6:7], 1.0e6)
             late["al"] = act([late["ar"], all_of("drr")], T.alpha[:], T.rr[:].indirect(T.al[:]))
         pending = []
@@ -268,19 +278,17 @@ def rank_program(g, core, T, topo):
         v_ra = tt([late["rs"], late["kc"]], T.ra[:], T.rs[:, 191:24 * 192:192], T.kcon[:], A.add)
         v_val = tt([s_z, c_cw], T.val[:], T.z2[:], T.cw[:], A.mult)
         a = tt([p_col, late["mn"]], T.cm[:], T.pb[:, 1536:1536 + C], T.maskn[:], A.mult)
-        a = scan([a, v_md, late["run"]], T.run[:, 16:16 + C], T.cm[:], T.mt0[:, 0:4 * C:4], 0.0, A.add, A.add)
+        a = scan([a, v_md, late["mz"]], T.run[:, 16:16 + C], T.mt0[:, 0:4 * C:4], T.cm[:], 0.0, A.add, A.subtract)
         a = tt([a], T.rkf[:], T.run[:, 31:16 + C:16], T.run[:, 15:C:16], A.subtract)
         a = tt([a, v_ra], T.rkf[:], T.rkf[:], T.ra[:], A.add)
         v_rl = copy([a], T.rl[:], T.rkf[:])
         if t == 0:
             late["qe"] = quant([c_et], T.qe[:], T.se[:], T.et[:])
-            fill([], T.bx[:, 0:1], 0.0)
-            late["bz"] = fill([], T.qk[:, K:K + 8], 9.0e5)
         p_f = [mm([late["qe"], t_h], T.pa[:, 512 * b:512 * b + C], T.qe[:, 128 * b:128 * b + 128], T.se[:, 128 * b:128 * b + 128], T.qx[:], T.sx[:]) for b in range(4)]
         v_w0 = copy([v_rl, v_val], T.w0[:].indirect(T.rl[:]), T.val[:])
         a = tt([v_w0, late["al"]], T.mm[:], T.w0[:], T.alpha[:], A.min)
         v_bx = scan([a], T.bx[:, 1:C], T.mm[:, 0:C - 1], T.mm[:, 0:C - 1], 0.0, A.max, A.max)
-        a = segments([v_bx, late["bz"], late["cw"]], T.bw, T.bx[:], T.lbf[:])
+        a = segments([v_bx, late["cw"]], T.bw, T.bx[:], T.lbf[:])
         v_lb = copy([a], T.lb[:, 0:24], T.lbf[:])
         s_fh = [act([p_f[b]], T.fh[:, C * b:C * b + C], T.pa[:, 512 * b:512 * b + C], None, 0.0, 0.5) for b in range(4)]
         s_wa = act([v_w0], T.wabs[:], T.w0[:], F.Abs)
@@ -291,7 +299,7 @@ def rank_program(g, core, T, topo):
         d_l4 = dma("s", [v_l4], T.l4[0:64, 16:26], T.l4[64:128, 0:10], "rc%d" % t)
         v_k0 = tt([s_wa, c_jw], T.kc[:, 0:C], T.wabs[:], T.jw[:], A.add)
         a = segments([v_k0], T.kw, T.kc[:, 1:321:2], T.ki[:])
-        a = ts([a], T.kj[:], T.ki[:], 511, None, A.bitwise_and)
+        a = ts([a], T.kj[:], T.ki[:], 1023, None, A.bitwise_and)
         v_l0 = copy([a], T.lp0[:], T.kj[:])
         f0 = []
         for b in range(4):
@@ -315,31 +323,35 @@ def rank_program(g, core, T, topo):
         k0, l0 = K * t, 56 * t
         ec, es, lc, ls = [T[k][:, k0:k0 + K] for k in ("ec", "es", "lc", "ls")]
         v_k = segments([v_p], T.kw, T.pl[:], T.ki[:])
-        a = ts([v_k], T.kp[:], T.ki[:], 9, None, A.arith_shift_right)
-        v_po = copy([a], T.po[:, l0:l0 + 10], T.kp[:])
-        d_po = rotate([v_po], T.po, 10, "rp%d" % t, l0)[3]
-        a = ts([v_k], T.kj[:], T.ki[:], 511, None, A.bitwise_and)
+        v_po = ts([v_k], T.po[:, l0:l0 + 10], T.ki[:], 2.0 ** -10, None, A.mult)
+        send([v_po], T.pi[:, l0:l0 + 10], T.po[:, l0:l0 + 10], "ap%d" % t)
+        a = ts([v_k], T.kj[:], T.ki[:], 1023, None, A.bitwise_and)
         v_lp = copy([a], T.lp[:], T.kj[:])
         e = [tt([v_lp, f0[b]], T.etile[:, b:4 * K:4], T.fh[:, C * b:C * b + C].indirect(T.lp[:]), T.fp0[:, K * b:K * b + K], A.add) for b in range(4)]
         v_ec = quant(e, ec, es, T.etile[:])
         send([v_ec], lc.bitcast(dt.uint8), ec.bitcast(dt.uint8), "ae%d" % t)
-        send([d_po], T.pi[:, l0:l0 + 50], T.po[:, l0:l0 + 50], "ap%d" % t)
         send([], ls, es, "ae%d" % t)
         if t == 0:
             late["ll"] = ts([c_ll, v_c0], T.ll[:], T.llf[:], T.cols[:, 0:1], None, A.add)
             late["qv"] = quant([t_vi], T.qv[:], T.sv[:], T.vt[:])
         s_fu = [act([p_f[b]], T.fu[:, C * b:C * b + C], T.pa[:, 512 * b:512 * b + C]) for b in range(4)]
         s_xb = [act([p_f[b], v_qx], T.xt[:, b:4 * C:4], T.pa[:, 512 * b:512 * b + C]) for b in range(4)]
+        d_pi = rotate([all_of("ap%d" % t)], T.pi, 10, "rp%d" % t, l0, True)
         a = copy([all_of("ap%d" % t), s_kc, v_kc], T.qk0[:], T.kc[:, 0:C].indirect(T.pi[:, l0:l0 + 10]))
         src = T.qk0
         for m in range(1, 5):
             dst = T.qk if m == 4 else (T.qk1, T.qk0)[(m - 1) % 2]
-            a = tt([a], dst[:, 0:K], T.kc[:, C * m:C * m + C].indirect(T.pi[:, l0 + 10 * m:l0 + 10 * m + 10]), src[:, 0:K], A.max)
+            a = tt([a, d_pi[m - 1]], dst[:, 0:K], T.kc[:, C * m:C * m + C].indirect(T.pi[:, l0 + 10 * m:l0 + 10 * m + 10]), src[:, 0:K], A.max)
             src = dst
         v_qk = a
-        v_kq = segments([v_qk], T.kw, T.qk[:, 0:K], T.kq[:])
-        v_oq = ts([v_kq], T.kj[:], T.kq[:], 511, None, A.bitwise_and)
+        a = scan([v_qk], T.kw[:], T.qk[:, 0:K], T.ctlw[:, 0:K], 1.0e6, A.min, A.max)
+        b_ = scan([], T.kw2[:], T.qk[:, 1:K + 1], T.ctlw[:, 0:K], 1.0e6, A.min, A.max)
+        v_kq = tt([a], T.kq[:], T.kw[:, 7:K:16], T.kw[:, 15:K:16], A.min)
+        b_ = tt([b_], T.kn[:], T.kw2[:, 7:K:16], T.kw2[:, 15:K:16], A.min)
+        v_oq = ts([v_kq], T.kj[:], T.kq[:], 1023, None, A.bitwise_and)
+        b_ = tt([b_], T.kn[:], T.kq[:], T.kn[:], A.is_equal)
         v_lv = copy([v_oq], T.lv[:], T.kj[:])
+        v_sp = tt([b_, c_sp], T.ds[:], T.kn[:], T.spare[:], A.mult)
         z = []
         for b in range(4):
             p_d = mm([all_of("ae%d" % t), v_val, v_rl], T.pb[:, 512 * b:512 * b + K], T.qe[:, 128 * b:128 * b + 128], T.se[:, 128 * b:128 * b + 128], lc, ls)
@@ -351,20 +363,20 @@ def rank_program(g, core, T, topo):
             p_h = mm([v_z, t_w, s_xb[3]], T.pa[:, 512 * b:512 * b + K], T.wq[:, 128 * b:128 * b + 128], T.wp[:, 128 * b:128 * b + 128], T.qz[:], T.sz[:])
             t_h = act([p_h], T.h16[:, K * b:K * b + K], T.pa[:, 512 * b:512 * b + K], None, 0.0, 0.0625)
             h.append(t_h)
-        v_kn = segments([v_qk, late["bz"]], T.kw2, T.qk[:, 1:K + 1], T.kn[:])
-        a = tt([v_kn, v_kq], T.kn[:], T.kq[:], T.kn[:], A.is_equal)
-        b_ = tt([v_oq, c_sp], T.ds[:], T.spare[:], T.kj[:], A.subtract)
-        a = tt([a, b_], T.ds[:], T.ds[:], T.kn[:], A.mult)
-        a = tt([a], T.ds[:], T.ds[:], T.kj[:], A.add)
+        a = tt([v_sp], T.ds[:], T.ds[:], T.kj[:], A.max)
         d = [ts([a], T.dl[:, 10 * b:10 * b + 10], T.ds[:], 4.0, float(b), A.mult, A.add) for b in range(4)]
         v_xs = None
-        n_ = [tt([v_lv, h[b], s_fu[b]], T.nt[:, K * b:K * b + K], T.fu[:, C * b:C * b + C].indirect(T.lv[:]), T.h16[:, K * b:K * b + K], A.add) for b in range(4)]
-        for b in range(4):
+        n_ = []
+        for i in (0, 1, -1, 2, -2, 3, -3, -4):
+            if i >= 0:
+                n_.append(tt([v_lv, h[i], s_fu[i]], T.nt[:, K * i:K * i + K], T.fu[:, C * i:C * i + C].indirect(T.lv[:]), T.h16[:, K * i:K * i + K], A.add))
+                continue
+            b = -1 - i
             v_xs = copy([n_[b], d[b], s_xb[3], v_xs], T.xt[:].indirect(T.dl[:, 10 * b:10 * b + 10]), T.nt[:, K * b:K * b + K])
         v_qx = quant([v_xs, p_f[3]], T.qx[:], T.sx[:], T.xt[:, 0:4 * C])
         if last:
             a = copy([v_qk], T.qi[:], T.qk[:, 0:K])
-            a = ts([a], T.qi[:], T.qi[:], 9, None, A.arith_shift_right)
+            a = ts([a], T.qi[:], T.qi[:], 10, None, A.arith_shift_right)
             a = ts([a], T.qf[:], T.qi[:], -1.0, 383.0, A.mult, A.add)
             v_lq = copy([a, late["ll"]], T.qo[:], T.qf[:].indirect(T.ll[:]))
 

from concourse.mybir import dt, AluOpType, ActivationFunctionType

C, K, R = 384, 160, 3
DIRECT = (23,)
MARK = 16
PART = 96
XW = 4 * 656
BIG = 1.0e29

SCRATCH = {
    "xt": ("sbuf", [128, XW], "bfloat16"), "qx": ("sbuf", [128, C], "float8_e4m3fn_x4"), "sx": ("sbuf", [128, C], "uint8"),
    "ut": ("sbuf", [128, 512], "bfloat16"), "vt": ("sbuf", [128, 512], "bfloat16"),
    "qu": ("sbuf", [128, 128], "float8_e4m3fn_x4"), "su": ("sbuf", [128, 128], "uint8"),
    "qa": ("sbuf", [128, 128], "float8_e4m3fn_x4"), "sa": ("sbuf", [128, 128], "uint8"),
    "qb": ("sbuf", [128, 128], "float8_e4m3fn_x4"), "sb": ("sbuf", [128, 128], "uint8"),
    "qv": ("sbuf", [128, 128], "float8_e4m3fn_x4"), "sv": ("sbuf", [128, 128], "uint8"),
    "wq": ("sbuf", [128, 512], "float8_e4m3fn_x4"), "wp": ("sbuf", [128, 512], "uint8"),
    "ones": ("sbuf", [128, 2048], "bfloat16"), "et": ("sbuf", [128, 2048], "bfloat16"),
    "qe": ("sbuf", [128, 512], "float8_e4m3fn_x4"), "se": ("sbuf", [128, 512], "uint8"),
    "ko": ("sbuf", [128, 512], "bfloat16"), "kot": ("sbuf", [128, 512], "bfloat16"),
    "qko": ("sbuf", [128, 128], "float8_e4m3fn_x4"), "sko": ("sbuf", [128, 128], "uint8"),
    "dq": ("sbuf", [128, C], "int32"), "ee": ("sbuf", [128, C], "float32"), "ff": ("sbuf", [128, C], "float32"),
    "maskb": ("sbuf", [128, C], "float32"), "maskn": ("sbuf", [128, C], "float32"), "ctl": ("sbuf", [128, C], "float32"),
    "ctlw": ("sbuf", [128, C], "float32"), "cw": ("sbuf", [128, C], "float32"), "jw": ("sbuf", [128, C], "float32"),
    "kcon": ("sbuf", [128, 24], "float32"), "cols": ("sbuf", [128, 8], "float32"), "r24": ("sbuf", [128, 2], "float32"),
    "ulf": ("sbuf", [128, 16], "float32"), "ul": ("sbuf", [128, 16], "uint16"),
    "alf": ("sbuf", [128, 24], "float32"), "al": ("sbuf", [128, 24], "uint16"),
    "llf": ("sbuf", [128, 10], "float32"), "ll": ("sbuf", [128, 10], "uint16"), "spare": ("sbuf", [128, 10], "int32"),
    "rvi": ("sbuf", [128, 24], "int32"), "rva": ("sbuf", [128, 24], "float32"),
    "rflat": ("dram", [8, C], "float32"), "rr": ("sbuf", [128, C], "float32"), "alpha": ("sbuf", [128, C], "float32"),
    "sm": ("sbuf", [128, C], "float32"), "sw": ("sbuf", [128, C], "float32"),
    "yy": ("sbuf", [128, 24 * C], "bfloat16"), "rs": ("sbuf", [128, 24 * 192], "bfloat16"),
    "ra": ("sbuf", [128, 24], "float32"), "cm": ("sbuf", [128, C], "float32"),
    "run": ("sbuf", [128, 16 + C], "float32"), "rkf": ("sbuf", [128, 24], "float32"), "rl": ("sbuf", [128, 24], "uint16"),
    "z1": ("sbuf", [128, C], "float32"), "z2": ("sbuf", [128, C], "float32"), "val": ("sbuf", [128, C], "float32"),
    "w0": ("sbuf", [128, C], "float32"), "wabs": ("sbuf", [128, C], "float32"), "mm": ("sbuf", [128, C], "float32"),
    "bx": ("sbuf", [128, C], "float32"), "bw": ("sbuf", [128, C], "float32"),
    "lbf": ("sbuf", [128, 24], "float32"), "lb": ("sbuf", [128, 120], "uint16"),
    "b4": ("sbuf", [128, K], "float32"), "l4f": ("sbuf", [128, 10], "float32"), "l4": ("sbuf", [128, 32], "uint16"),
    "kc": ("sbuf", [128, 5 * C], "float32"),
    "kw": ("sbuf", [128, K], "float32"), "ki": ("sbuf", [128, 10], "int32"), "kj": ("sbuf", [128, 10], "int32"),
    "lp0": ("sbuf", [128, 10], "uint16"), "lp": ("sbuf", [128, 10], "uint16"), "lv": ("sbuf", [128, 10], "uint16"),
    "kp": ("sbuf", [128, 10], "int32"), "pk": ("sbuf", [128, K], "float32"), "pl": ("sbuf", [128, K], "float32"),
    "qk0": ("sbuf", [128, K], "float32"), "qk1": ("sbuf", [128, K], "float32"), "qk": ("sbuf", [128, K + 8], "float32"),
    "kw2": ("sbuf", [128, K], "float32"), "kn": ("sbuf", [128, 10], "int32"), "kq": ("sbuf", [128, 10], "int32"),
    "ds": ("sbuf", [128, 10], "int32"), "dl": ("sbuf", [128, 40], "uint16"),
    "qi": ("sbuf", [128, K], "int32"), "qf": ("sbuf", [128, K], "float32"), "qo": ("sbuf", [128, K], "float32"),
    "fh": ("sbuf", [128, 4 * C], "bfloat16"), "fu": ("sbuf", [128, 4 * C], "bfloat16"),
    "fp0": ("sbuf", [128, 4 * K], "bfloat16"), "etile": ("sbuf", [128, 4 * K], "bfloat16"),
    "vtile": ("sbuf", [128, 4 * K], "bfloat16"), "qz": ("sbuf", [128, K], "float8_e4m3fn_x4"), "sz": ("sbuf", [128, K], "uint8"),
    "de": ("sbuf", [128, 4 * K], "float32"), "h16": ("sbuf", [128, 4 * K], "float32"), "nt": ("sbuf", [128, 4 * K], "bfloat16"),
    "yo": ("sbuf", [128, C], "float32"),
    "pa": ("psum", [128, 2048], "float32"), "pb": ("psum", [128, 2048], "float32"),
}
TILES = [(384, (0, 23, 22, 21)), (320, (20, 19, 18, 17)), (256, (16, 15, 14, 13)), (192, (12, 11, 10, 9)), (128, (8, 7, 6, 5)), (128, (4, 3, 2, 1))]
for _q, (_n, _s) in enumerate(TILES):
    SCRATCH["mt%d" % _q] = ("sbuf", [128, 4 * _n], "bfloat16")
    SCRATCH["qm%d" % _q] = ("sbuf", [128, _n], "float8_e4m3fn_x4")
    SCRATCH["sm%d" % _q] = ("sbuf", [128, _n], "uint8")
SCRATCH["ec"] = SCRATCH["lc"] = ("sbuf", [128, R * K], "float8_e4m3fn_x4")
SCRATCH["es"] = SCRATCH["ls"] = ("sbuf", [128, R * K], "uint8")
SCRATCH["po"] = SCRATCH["pi"] = ("sbuf", [128, R * 56], "uint16")

SEMAPHORES = ["v", "s", "t", "p", "dx", "du", "dw", "dv", "drv", "drf", "drr", "dout", "ls"]
SEMAPHORES += ["%s%d" % (a, t) for a in ("ae", "ap", "rc") for t in range(R)]
SEMAPHORES += ["%s%d%d" % (a, t, m) for a in ("rb", "rp") for t in range(R) for m in range(1, 5)]


def rank_program(g, core, T, topo):
    rank = T.rank_of(core)
    if rank is None:
        return
    A, F = AluOpType, ActivationFunctionType
    eng = {"v": g.vector, "s": g.scalar, "t": g.tensor, "p": g, "y": g.sync}
    cnt, seen = {}, {}

    def need(q, toks):
        best = {}
        for k in toks:
            if k is not None:
                best[k[0]] = max(best.get(k[0], 0), k[1])
        for s, n in best.items():
            if seen.get((q, s), 0) < n:
                eng[q].wait_ge(T.sem[s], n)
                seen[(q, s)] = n

    def done(ins, sem, n=1):
        ins.then_inc(T.sem[sem], n)
        cnt[sem] = cnt.get(sem, 0) + n
        return (sem, cnt[sem])

    def all_of(sem):
        return (sem, cnt[sem])

    def copy(deps, out, in_):
        need("v", deps)
        return done(g.vector.tensor_copy(out, in_), "v")

    def tt(deps, out, a, b, op):
        need("v", deps)
        return done(g.vector.tensor_tensor(out, a, b, op), "v")

    def ts(deps, out, a, s1, s2, op0, op1=None):
        need("v", deps)
        if op1 is None:
            return done(g.vector.tensor_scalar(out, a, s1, None, op0), "v")
        return done(g.vector.tensor_scalar(out, a, s1, s2, op0, op1), "v")

    def scan(deps, out, d0, d1, init, op0, op1):
        need("v", deps)
        return done(g.vector.tensor_tensor_scan(out, d0, d1, init, op0, op1), "v")

    def fill(deps, out, c):
        need("v", deps)
        return done(g.vector.memset(out, c), "v")

    def quant(deps, q, s, x):
        need("v", deps)
        return done(g.vector.quantize_mx(q, s, x), "v")

    def act(deps, out, in_, func=None, bias=0.0, scale=1.0):
        need("s", deps)
        f = F.Copy if func is None else func
        if func is None and scale == 1.0:
            return done(g.scalar.activation(out, in_, f), "s")
        if func is None:
            return done(g.scalar.activation(out, in_, f, scale=scale), "s")
        return done(g.scalar.activation(out, in_, f, bias=bias, scale=scale), "s")

    def mm(deps, out, w, ws, x, xs, start=True, stop=True):
        need("t", deps)
        return done(g.tensor.matmul_mx(out, w, ws, x, xs, start, stop), "t")

    def iota(out, pattern, base, cm):
        return done(g.iota(out, pattern, base, cm, allow_small_or_imprecise_dtypes=True), "p")

    def dma(q, deps, out, in_, sem):
        need(q, deps)
        return done(eng[q].dma_start(out, in_), sem, 16)

    def rotate(deps, buf, w, sem, o=0, each=False):
        tok = []
        for m in range(1, 5):
            z, d = sem + (str(m) if each else ""), o + w * m
            dma("y", deps, buf[16 * m:128, d:d + w], buf[0:128 - 16 * m, o:o + w], z)
            tok.append(dma("s", deps, buf[0:16 * m, d:d + w], buf[128 - 16 * m:128, o:o + w], z))
        return tok

    def segments(deps, scratch, src, out):
        n = 16 * out.shape[1]
        a = scan(deps, scratch[:, 0:n], src, T.ctlw[:, 0:n], 1.0e6, A.min, A.max)
        return tt([a], out, scratch[:, 7:n:16], scratch[:, 15:n:16], A.min)

    t_u = dma("s", [], T.ut[:], T.u[:], "du")
    t_x = dma("y", [], T.xt[:, 0:4 * C], T.x[:], "dx")
    t_rv = dma("s", [], T.rvi[:], T.rv[:], "drv")
    dma("y", [], T.wq[:].bitcast(dt.uint8), T.wc[:], "dw")
    t_w = dma("y", [], T.wp[:], T.ws[:], "dw")
    t_vi = dma("y", [], T.vt[:], T.v[:], "dv")

    c_ul = iota(T.ulf[:], [[8, 2], [16, 8]], 0, 0)
    c_dq = iota(T.dq[:], [[1, C]], 128, -1)
    c_ee = iota(T.ee[:], [[0, 24], [1, 16]], 0, 0)
    c_kc = iota(T.kcon[:], [[-16, 24]], 575, 0)
    v_one = fill([], T.ones[:], 1.0)
    late = {}
    for q, (n, segs) in enumerate(TILES):
        o, w = 64 * min(k for k in segs if k), 4 * n
        act([v_one], T["mt%d" % q][:, o:w], T.ones[:, o:w], None, 0.0, 0.0)
    act([], T.rs[:, 191:192], T.ones[:, 0:1], None, 0.0, -192.0)
    act([], T.run[:, 0:16], T.ones[:, 0:16], None, 0.0, 0.0)
    act([], T.bx[:, 0:1], T.ones[:, 0:1], None, 0.0, 0.0)
    late["mz"] = act([], T.qk[:, K:K + 8], T.ones[:, 0:8], None, 0.0, 9.0e5)
    need("p", [v_one])
    a = done(g.affine_select(T.kot[:], T.ones[:, 0:512], [[-16, 8], [0, 64]], A.is_ge, 0.0, 0, 1), "p")
    need("p", [a])
    c_ko = done(g.affine_select(T.ko[:], T.kot[:], [[16, 8], [0, 64]], A.is_ge, 0.0, 15, -1), "p")
    c_al = iota(T.alf[:], [[-1, 24]], 23, 0)
    c_ll = iota(T.llf[:], [[-16, 10]], 144, 0)
    c_sp = iota(T.spare[:], [[16, 10]], C, 1)
    c_cw = iota(T.cw[:], [[1, C]], 512, 0)
    c_et = done(g.affine_select(T.et[:], T.ones[:], [[-1, 4], [1, 512]], A.is_equal, 0.0, 0, -4), "p")
    c_jw = iota(T.jw[:], [[1024, C]], -512, 0)

    v_ul = copy([c_ul], T.ul[:], T.ulf[:])
    v_dq = ts([c_dq], T.dq[:], T.dq[:], 15, None, A.bitwise_and)
    v_mb = ts([v_dq], T.maskb[:], T.dq[:], 0.5, -2.0 * BIG, A.subtract, A.mult)
    late["mn"] = ts([v_dq], T.maskn[:], T.dq[:], 0.0, None, A.is_equal)
    v_c0 = copy([v_dq], T.cols[:, 0:1], T.dq[:, 15:16])
    v_qu = quant([t_u], T.qu[:], T.su[:], T.ut[:])
    for q, s, a in ((T.qa, T.sa, 0), (T.qb, T.sb, 8)):
        v_pick = copy([v_qu, v_ul], q[:].bitcast(dt.uint32), T.qu[:].bitcast(dt.uint32).indirect(T.ul[:, a:a + 8]))
        s_pick = act([v_qu, v_ul], s[:], T.su[:].indirect(T.ul[:, a:a + 8]))
    v_qx = quant([t_x], T.qx[:], T.sx[:], T.xt[:, 0:4 * C])
    v_ct = ts([c_ee], T.ctl[:], T.ee[:], 0.5, 2.0 * BIG, A.subtract, A.mult)

    def constants_early():
        k = [T.cols[:, i:i + 1] for i in range(8)]
        r = act([v_c0], k[1], k[0], F.Identity, 15.0, -1.0)
        late["ar"] = act([], T.r24[:, 0:1], k[0], None, 0.0, 24.0)
        a = act([], k[7], k[0], None, 0.0, -1.0)
        late["kc"] = act([a, c_kc], T.kcon[:], T.kcon[:], F.Identity, k[7])
        a = act([r], k[2], k[1], F.Sign, -7.5)
        a = act([a], k[3], k[2], F.Identity, 4.0, 4.0)
        b = act([a], k[4], k[3], F.Identity, k[1])
        c = act([a], k[5], k[1], F.Identity, k[3], -1.0)
        b = act([b], k[2], k[4], F.Identity, -3.5, -0.5)
        c = act([c], k[6], k[5], F.Identity, -3.75e6, -0.5e6)
        late["b"] = c

    def constants_lists():
        a = ts([t_rv], T.rva[:], T.rvi[:], 1.0, 384.0, A.max, A.subtract)
        a = ts([a], T.rva[:], T.rva[:], -1.0, None, A.mult)
        t_rf = dma("y", [a], T.rflat[:], T.rva[:], "drf")
        for q in range(16):
            dma("y", [t_rf], T.rr[q:128:16, :], T.rflat[:], "drr")
        late["ar"] = ts([late["ar"], c_al], T.al[:], T.alf[:], T.r24[:, 0:1], None, A.add)
        late["ko"] = quant([c_ko], T.qko[:], T.sko[:], T.ko[:])

    nxt = T.cores[(rank + 1) % len(T.cores)]
    rid, pid = topo.addr(nxt)[0:2]
    mask, ne = topo.mask(core, nxt), len(topo.engines(core, nxt))

    def send(deps, out, in_, sem):
        need("p", deps)
        g.remote_dma(out, in_, T.sem[sem], T.sem.ls, pid, rid, mask)
        cnt["ls"] = cnt.get("ls", 0) + ne
        cnt[sem] = cnt.get(sem, 0) + ne

    t_h = t_de = None
    for t in range(R):
        last = t == R - 1
        p_s1 = mm([v_qx, v_pick, s_pick, t_de], T.pb[:, 0:C], T.qa[:], T.sa[:], T.qx[:], T.sx[:])
        p_s2 = mm([], T.pb[:, 512:512 + C], T.qa[:], T.sa[:], T.qx[:], T.sx[:])
        p_mk = mm([], T.pb[:, 1024:1024 + C], T.qb[:], T.sb[:], T.qx[:], T.sx[:])
        a = tt([p_s1, v_mb], T.sm[:], T.pb[:, 0:C], T.maskb[:], A.min)
        v_sw = scan([a, v_ct], T.sw[:], T.ctl[:], T.sm[:], -BIG, A.min, A.max)
        if t == 0:
            constants_early()
            constants_lists()
        y = {}
        for i, k in enumerate(k for n, segs in TILES for k in segs if k):
            if i == MARK:
                a = act([p_mk], T.z1[:], T.pb[:, 1024:1024 + C], F.Sign)
                s_z = act([a], T.z2[:], T.z1[:], F.Sign, -1.0, 2.0)
            if k in DIRECT:
                continue
            y[k] = act([p_s2, v_sw], T.yy[:, C * k:C * k + 16 * k], T.pb[:, 512:512 + 16 * k], F.Sign, T.sw[:, 16 * k + 15:16 * k + 16], -1.0)
        if t == 0:
            a = act([late["b"], c_ee], T.ff[:], T.ee[:], F.Abs, T.cols[:, 2:3])
            late["cw"] = act([a], T.ctlw[:], T.ff[:], F.Identity, T.cols[:, 6:7], 1.0e6)
            late["al"] = act([late["ar"], all_of("drr")], T.alpha[:], T.rr[:].indirect(T.al[:]))
        pending = []

        def flush():
            while pending:
                m, e, k, tok = pending.pop()
                late["rs"] = scan(tok, T.rs[:, 192 * k + 192 - 8 * k:192 * k + 192], m[:, e:32 * k:4], m[:, 32 * k + e:64 * k:4], -192.0, A.add, A.add)

        for q, (n, segs) in enumerate(TILES):
            m, ok = T["mt%d" % q], [late["mz"]]
            for e, k in enumerate(segs):
                if k == 0:
                    ok.append(tt([v_sw], m[:, 0:4 * C:4], T.pb[:, 0:C], T.sw[:], A.is_le))
                    v_md = ok[-1]
                    continue
                if k in DIRECT:
                    a = ts([v_sw], m[:, e:64 * k:4], T.pb[:, 0:16 * k], T.sw[:, 16 * k + 15:16 * k + 16], None, A.is_lt)
                else:
                    a = ts([y[k]], m[:, e:64 * k:4], T.yy[:, C * k:C * k + 16 * k], 0.0, None, A.is_gt)
                ok.append(a)
                flush()
                pending.append((m, e, k, [a]))
            if q == 5:
                flush()
            v_qm = quant(ok, T["qm%d" % q][:], T["sm%d" % q][:], m[:])
            p_col = mm([v_qm, late["ko"], t_de], T.pb[:, 1536:1536 + n], T.qko[:], T.sko[:], T["qm%d" % q][:], T["sm%d" % q][:], q == 0, q == 5)
        v_ra = tt([late["rs"], late["kc"]], T.ra[:], T.rs[:, 191:24 * 192:192], T.kcon[:], A.add)
        v_val = tt([s_z, c_cw], T.val[:], T.z2[:], T.cw[:], A.mult)
        a = tt([p_col, late["mn"]], T.cm[:], T.pb[:, 1536:1536 + C], T.maskn[:], A.mult)
        a = scan([a, v_md, late["mz"]], T.run[:, 16:16 + C], T.mt0[:, 0:4 * C:4], T.cm[:], 0.0, A.add, A.subtract)
        a = tt([a], T.rkf[:], T.run[:, 31:16 + C:16], T.run[:, 15:C:16], A.subtract)
        a = tt([a, v_ra], T.rkf[:], T.rkf[:], T.ra[:], A.add)
        v_rl = copy([a], T.rl[:], T.rkf[:])
        if t == 0:
            late["qe"] = quant([c_et], T.qe[:], T.se[:], T.et[:])
        p_f = [mm([late["qe"], t_h], T.pa[:, 512 * b:512 * b + C], T.qe[:, 128 * b:128 * b + 128], T.se[:, 128 * b:128 * b + 128], T.qx[:], T.sx[:]) for b in range(4)]
        v_w0 = copy([v_rl, v_val], T.w0[:].indirect(T.rl[:]), T.val[:])
        a = tt([v_w0, late["al"]], T.mm[:], T.w0[:], T.alpha[:], A.min)
        v_bx = scan([a], T.bx[:, 1:C], T.mm[:, 0:C - 1], T.mm[:, 0:C - 1], 0.0, A.max, A.max)
        a = segments([v_bx, late["cw"]], T.bw, T.bx[:], T.lbf[:])
        v_lb = copy([a], T.lb[:, 0:24], T.lbf[:])
        s_fh = [act([p_f[b]], T.fh[:, C * b:C * b + C], T.pa[:, 512 * b:512 * b + C], None, 0.0, 0.5) for b in range(4)]
        s_wa = act([v_w0], T.wabs[:], T.w0[:], F.Abs)
        d_lb = rotate([v_lb], T.lb, 24, "rb%d" % t, 0, True)
        a = segments([v_bx], T.b4, T.bx[:, 1:321:2], T.l4f[:])
        v_l4 = copy([a], T.l4[:, 0:10], T.l4f[:])
        dma("y", [v_l4], T.l4[64:128, 16:26], T.l4[0:64, 0:10], "rc%d" % t)
        d_l4 = dma("s", [v_l4], T.l4[0:64, 16:26], T.l4[64:128, 0:10], "rc%d" % t)
        v_k0 = tt([s_wa, c_jw], T.kc[:, 0:C], T.wabs[:], T.jw[:], A.add)
        a = segments([v_k0], T.kw, T.kc[:, 1:321:2], T.ki[:])
        a = ts([a], T.kj[:], T.ki[:], 1023, None, A.bitwise_and)
        v_l0 = copy([a], T.lp0[:], T.kj[:])
        f0 = []
        for b in range(4):
            w, o = T.fh[:, C * b:C * b + C].indirect(T.lp0[:]), T.fp0[:, K * b:K * b + K]
            f0.append(copy([v_l0, s_fh[b]], o, w) if b < 2 else act([v_l0, s_fh[b]], o, w))
        acc = T.kc[:, 1:321:2]
        s_kc = v_kc = before = v_k0
        v_p = None
        for m in range(1, 5):
            pt = PART if m < 4 else 0
            w, l = T.kc[:, C * (m - 1):C * m], 24 * m
            if pt:
                v_kc = copy([d_lb[m - 1], s_kc, v_kc], T.kc[:, C * m:C * m + pt], w.indirect(T.lb[:, l:l + pt // 16]))
            s_kc = act([d_lb[m - 1], s_kc, before], T.kc[:, C * m + pt:C * m + C], w.indirect(T.lb[:, l + pt // 16:l + 24]))
            before = v_kc
            if m < 4:
                v_p = tt([s_kc, v_kc, v_p], T.pk[:], acc, T.kc[:, C * m + 1:C * m + 321:2], A.max)
                acc = T.pk[:]
            if m == 3:
                v_p = tt([v_p, d_l4], T.pl[:], T.kc[:, C * m:C * m + C].indirect(T.l4[:, 16:26]), T.pk[:], A.max)
        k0, l0 = K * t, 56 * t
        ec, es, lc, ls = [T[k][:, k0:k0 + K] for k in ("ec", "es", "lc", "ls")]
        v_k = segments([v_p], T.kw, T.pl[:], T.ki[:])
        v_po = ts([v_k], T.po[:, l0:l0 + 10], T.ki[:], 2.0 ** -10, None, A.mult)
        send([v_po], T.pi[:, l0:l0 + 10], T.po[:, l0:l0 + 10], "ap%d" % t)
        a = ts([v_k], T.kj[:], T.ki[:], 1023, None, A.bitwise_and)
        v_lp = copy([a], T.lp[:], T.kj[:])
        e = [tt([v_lp, f0[b]], T.etile[:, b:4 * K:4], T.fh[:, C * b:C * b + C].indirect(T.lp[:]), T.fp0[:, K * b:K * b + K], A.add) for b in range(4)]
        v_ec = quant(e, ec, es, T.etile[:])
        send([v_ec], lc.bitcast(dt.uint8), ec.bitcast(dt.uint8), "ae%d" % t)
        send([], ls, es, "ae%d" % t)
        if t == 0:
            late["ll"] = ts([c_ll, v_c0], T.ll[:], T.llf[:], T.cols[:, 0:1], None, A.add)
            late["qv"] = quant([t_vi], T.qv[:], T.sv[:], T.vt[:])
        s_fu = [act([p_f[b]], T.fu[:, C * b:C * b + C], T.pa[:, 512 * b:512 * b + C]) for b in range(4)]
        s_xb = [act([p_f[b], v_qx], T.xt[:, b:4 * C:4], T.pa[:, 512 * b:512 * b + C]) for b in range(4)]
        d_pi = rotate([all_of("ap%d" % t)], T.pi, 10, "rp%d" % t, l0, True)
        a = copy([all_of("ap%d" % t), s_kc, v_kc], T.qk0[:], T.kc[:, 0:C].indirect(T.pi[:, l0:l0 + 10]))
        src = T.qk0
        for m in range(1, 5):
            dst = T.qk if m == 4 else (T.qk1, T.qk0)[(m - 1) % 2]
            a = tt([a, d_pi[m - 1]], dst[:, 0:K], T.kc[:, C * m:C * m + C].indirect(T.pi[:, l0 + 10 * m:l0 + 10 * m + 10]), src[:, 0:K], A.max)
            src = dst
        v_qk = a
        a = scan([v_qk], T.kw[:], T.qk[:, 0:K], T.ctlw[:, 0:K], 1.0e6, A.min, A.max)
        b_ = scan([], T.kw2[:], T.qk[:, 1:K + 1], T.ctlw[:, 0:K], 1.0e6, A.min, A.max)
        v_kq = tt([a], T.kq[:], T.kw[:, 7:K:16], T.kw[:, 15:K:16], A.min)
        b_ = tt([b_], T.kn[:], T.kw2[:, 7:K:16], T.kw2[:, 15:K:16], A.min)
        v_oq = ts([v_kq], T.kj[:], T.kq[:], 1023, None, A.bitwise_and)
        b_ = tt([b_], T.kn[:], T.kq[:], T.kn[:], A.is_equal)
        v_lv = copy([v_oq], T.lv[:], T.kj[:])
        v_sp = tt([b_, c_sp], T.ds[:], T.kn[:], T.spare[:], A.mult)
        z = []
        for b in range(4):
            p_d = mm([all_of("ae%d" % t), v_val, v_rl], T.pb[:, 512 * b:512 * b + K], T.qe[:, 128 * b:128 * b + 128], T.se[:, 128 * b:128 * b + 128], lc, ls)
            t_de = act([p_d], T.de[:, K * b:K * b + K], T.pb[:, 512 * b:512 * b + K], None, 0.0, 0.5)
            z.append(tt([v_lv, t_de], T.vtile[:, b:4 * K:4], T.fh[:, C * b:C * b + C].indirect(T.lv[:]), T.de[:, K * b:K * b + K], A.add))
        v_z = quant(z, T.qz[:], T.sz[:], T.vtile[:])
        h = []
        for b in range(4):
            p_h = mm([v_z, t_w, s_xb[3]], T.pa[:, 512 * b:512 * b + K], T.wq[:, 128 * b:128 * b + 128], T.wp[:, 128 * b:128 * b + 128], T.qz[:], T.sz[:])
            t_h = act([p_h], T.h16[:, K * b:K * b + K], T.pa[:, 512 * b:512 * b + K], None, 0.0, 0.0625)
            h.append(t_h)
        a = tt([v_sp], T.ds[:], T.ds[:], T.kj[:], A.max)
        d = [ts([a], T.dl[:, 10 * b:10 * b + 10], T.ds[:], 4.0, float(b), A.mult, A.add) for b in range(4)]
        v_xs = None
        n_ = []
        for i in (0, 1, -1, 2, -2, 3, -3, -4):
            if i >= 0:
                n_.append(tt([v_lv, h[i], s_fu[i]], T.nt[:, K * i:K * i + K], T.fu[:, C * i:C * i + C].indirect(T.lv[:]), T.h16[:, K * i:K * i + K], A.add))
                continue
            b = -1 - i
            v_xs = copy([n_[b], d[b], s_xb[3], v_xs], T.xt[:].indirect(T.dl[:, 10 * b:10 * b + 10]), T.nt[:, K * b:K * b + K])
        v_qx = quant([v_xs, p_f[3]], T.qx[:], T.sx[:], T.xt[:, 0:4 * C])
        if last:
            a = copy([v_qk], T.qi[:], T.qk[:, 0:K])
            a = ts([a], T.qi[:], T.qi[:], 10, None, A.arith_shift_right)
            a = ts([a], T.qf[:], T.qi[:], -1.0, 383.0, A.mult, A.add)
            v_lq = copy([a, late["ll"]], T.qo[:], T.qf[:].indirect(T.ll[:]))

    dma("y", [v_qx], T.oc[:], T.qx[:].bitcast(dt.uint8), "dout")
    for k in range(4):
        dma("s" if k % 2 else "y", [v_qx], T.osc[4 * k:4 * k + 4, :], T.sx[32 * k:32 * k + 4, :], "dout")
    p_y = mm([v_qx, late["qv"], t_de], T.pb[:, 0:C], T.qv[:], T.sv[:], T.qx[:], T.sx[:])
    s_y = act([p_y], T.yo[:], T.pb[:, 0:C])
    for q in range(8):
        dma("y", [v_lq], T.lq[q:q + 1, :], T.qo[16 * q:16 * q + 1, :], "dout")
    dma("s", [s_y], T.y[:], T.yo[:], "dout")
    need("p", [all_of(s) for s in cnt])
